import numpy as np
import ml_dtypes

BF16 = ml_dtypes.bfloat16


def bf(x):
    return np.asarray(x, np.float32).astype(BF16)


def f32(x):
    return np.asarray(x, np.float32)


def f64(x):
    return np.asarray(x).astype(np.float64)


def striped(idx):
    return np.tile(idx.reshape(-1, 16).T, (8, 1))


S, K, M, N, D, V = 512, 256, 256, 256, 4, 64


def setup_inputs():
    return {"table": bf(np.random.standard_normal((K, S))), "w": bf(np.random.standard_normal((K, M)) / np.sqrt(D * K)), "s": f32(0.5 + np.random.random_sample((M, 1))), "b": f32(0.5 * np.random.standard_normal((M, 1))), "offs": striped(np.random.permutation(S)[:N])}


def reference(table, w, s, b, offs):
    idx = offs[:16].T.reshape(-1)
    x = f64(table)[:, idx]
    y = f64(w).T @ sum(x[:, t * V : (t + 1) * V] for t in range(D))
    return y * f64(s) + f64(b)

@@ -1,0 +1,63 @@
+import concourse.mybir as mybir
+
+P = 128
+S = 512
+K = 256
+M = 256
+NEIGHBOURS = 4
+NODES = 64
+K_BLOCKS = K // P
+M_BLOCKS = M // P
+PIECE_COLUMNS = NODES // 16
+
+FLOPS = 2 * K * M * NODES + (NEIGHBOURS - 1) * K * NODES + 2 * M * NODES
+
+BF16 = mybir.dt.bfloat16
+F32 = mybir.dt.float32
+U16 = mybir.dt.uint16
+MULT = mybir.AluOpType.mult
+ADD = mybir.AluOpType.add
+
+
+def tile_gather_matmul_kernel(tc, table, w, s, b, offs, out):
+    nc = tc.nc
+    with (
+        tc.tile_pool(name="held", bufs=1) as held,
+        tc.psum_pool(name="psum", bufs=1) as psum,
+    ):
+        offsets = held.tile([P, NEIGHBOURS * PIECE_COLUMNS], U16, name="offsets")
+        nc.sync.dma_start(offsets[:], offs)
+
+        table_blocks = [held.tile([P, S], BF16, name=f"table{kb}") for kb in range(K_BLOCKS)]
+        w_blocks = [held.tile([P, M], BF16, name=f"w{kb}") for kb in range(K_BLOCKS)]
+        for kb in range(K_BLOCKS):
+            rows = slice(kb * P, (kb + 1) * P)
+            nc.sync.dma_start(table_blocks[kb][:], table[rows, :])
+            nc.scalar.dma_start(w_blocks[kb][:], w[rows, :])
+
+        gain = held.tile([P, M_BLOCKS], F32, name="gain")
+        shift = held.tile([P, M_BLOCKS], F32, name="shift")
+        with nc.allow_non_contiguous_dma(reason="one float32 to a partition"):
+            nc.gpsimd.dma_start(gain[:], s.rearrange("(a p) o -> p (a o)", p=P))
+            nc.gpsimd.dma_start(shift[:], b.rearrange("(a p) o -> p (a o)", p=P))
+
+        banks = [psum.tile([P, NODES], F32, name=f"bank{mb}") for mb in range(M_BLOCKS)]
+        for kb in range(K_BLOCKS):
+            for mb in range(M_BLOCKS):
+                for t in range(NEIGHBOURS):
+                    piece = offsets[:, t * PIECE_COLUMNS : (t + 1) * PIECE_COLUMNS]
+                    nc.tensor.matmul(
+                        banks[mb][:],
+                        w_blocks[kb][:, mb * P : (mb + 1) * P],
+                        table_blocks[kb][:].indirect(piece),
+                        start=(kb == 0 and t == 0),
+                        stop=(kb == K_BLOCKS - 1 and t == NEIGHBOURS - 1),
+                    )
+
+        store_queues = [nc.sync, nc.scalar]
+        for mb in range(M_BLOCKS):
+            result = held.tile([P, NODES], F32, name=f"result{mb}")
+            nc.vector.tensor_scalar(
+                result[:], banks[mb][:], gain[:, mb : mb + 1], shift[:, mb : mb + 1], MULT, ADD
+            )
+            store_queues[mb].dma_start(out[mb * P : (mb + 1) * P, :], result[:])

@@ -9,6 +9,8 @@ NODES = 64
 K_BLOCKS = K // P
 M_BLOCKS = M // P
 PIECE_COLUMNS = NODES // 16
+BANK = 512
+WARM_UP_MATMULS = 5
 
 FLOPS = 2 * K * M * NODES + (NEIGHBOURS - 1) * K * NODES + 2 * M * NODES
 
@@ -25,6 +27,12 @@ def tile_gather_matmul_kernel(tc, table, w, s, b, offs, out):
         tc.tile_pool(name="held", bufs=1) as held,
         tc.psum_pool(name="psum", bufs=1) as psum,
     ):
+        zeros = held.tile([P, BANK], BF16, name="zeros")
+        nc.vector.memset(zeros[:], 0.0)
+        idle_bank = psum.tile([P, BANK], F32, name="idle_bank")
+        for i in range(WARM_UP_MATMULS):
+            nc.tensor.matmul(idle_bank[:], zeros[:, 0:P], zeros[:], start=True, stop=True)
+
         offsets = held.tile([P, NEIGHBOURS * PIECE_COLUMNS], U16, name="offsets")
         nc.sync.dma_start(offsets[:], offs)
 

@@ -9,8 +9,6 @@ NODES = 64
 K_BLOCKS = K // P
 M_BLOCKS = M // P
 PIECE_COLUMNS = NODES // 16
-BANK = 512
-WARM_UP_MATMULS = 5
 
 FLOPS = 2 * K * M * NODES + (NEIGHBOURS - 1) * K * NODES + 2 * M * NODES
 
@@ -27,12 +25,6 @@ def tile_gather_matmul_kernel(tc, table, w, s, b, offs, out):
         tc.tile_pool(name="held", bufs=1) as held,
         tc.psum_pool(name="psum", bufs=1) as psum,
     ):
-        zeros = held.tile([P, BANK], BF16, name="zeros")
-        nc.vector.memset(zeros[:], 0.0)
-        idle_bank = psum.tile([P, BANK], F32, name="idle_bank")
-        for i in range(WARM_UP_MATMULS):
-            nc.tensor.matmul(idle_bank[:], zeros[:, 0:P], zeros[:], start=True, stop=True)
-
         offsets = held.tile([P, NEIGHBOURS * PIECE_COLUMNS], U16, name="offsets")
         nc.sync.dma_start(offsets[:], offs)
 
@@ -46,8 +38,8 @@ def tile_gather_matmul_kernel(tc, table, w, s, b, offs, out):
         gain = held.tile([P, M_BLOCKS], F32, name="gain")
         shift = held.tile([P, M_BLOCKS], F32, name="shift")
         with nc.allow_non_contiguous_dma(reason="one float32 to a partition"):
-            nc.gpsimd.dma_start(gain[:], s.rearrange("(a p) o -> p (a o)", p=P))
-            nc.gpsimd.dma_start(shift[:], b.rearrange("(a p) o -> p (a o)", p=P))
+            nc.scalar.dma_start(gain[:], s.rearrange("(a p) o -> p (a o)", p=P))
+            nc.scalar.dma_start(shift[:], b.rearrange("(a p) o -> p (a o)", p=P))
 
         banks = [psum.tile([P, NODES], F32, name=f"bank{mb}") for mb in range(M_BLOCKS)]
         for kb in range(K_BLOCKS):

@@ -6,9 +6,9 @@ K = 256
 M = 256
 NEIGHBOURS = 4
 NODES = 64
+LIST = NEIGHBOURS * NODES
 K_BLOCKS = K // P
 M_BLOCKS = M // P
-PIECE_COLUMNS = NODES // 16
 
 FLOPS = 2 * K * M * NODES + (NEIGHBOURS - 1) * K * NODES + 2 * M * NODES
 
@@ -17,6 +17,7 @@ F32 = mybir.dt.float32
 U16 = mybir.dt.uint16
 MULT = mybir.AluOpType.mult
 ADD = mybir.AluOpType.add
+X = mybir.AxisListType.X
 
 
 def tile_gather_matmul_kernel(tc, table, w, s, b, offs, out):
@@ -25,7 +26,7 @@ def tile_gather_matmul_kernel(tc, table, w, s, b, offs, out):
         tc.tile_pool(name="held", bufs=1) as held,
         tc.psum_pool(name="psum", bufs=1) as psum,
     ):
-        offsets = held.tile([P, NEIGHBOURS * PIECE_COLUMNS], U16, name="offsets")
+        offsets = held.tile([P, LIST // 16], U16, name="offsets")
         nc.sync.dma_start(offsets[:], offs)
 
         table_blocks = [held.tile([P, S], BF16, name=f"table{kb}") for kb in range(K_BLOCKS)]
@@ -38,26 +39,26 @@ def tile_gather_matmul_kernel(tc, table, w, s, b, offs, out):
         gain = held.tile([P, M_BLOCKS], F32, name="gain")
         shift = held.tile([P, M_BLOCKS], F32, name="shift")
         with nc.allow_non_contiguous_dma(reason="one float32 to a partition"):
-            nc.scalar.dma_start(gain[:], s.rearrange("(a p) o -> p (a o)", p=P))
-            nc.scalar.dma_start(shift[:], b.rearrange("(a p) o -> p (a o)", p=P))
-
-        banks = [psum.tile([P, NODES], F32, name=f"bank{mb}") for mb in range(M_BLOCKS)]
-        for kb in range(K_BLOCKS):
-            for mb in range(M_BLOCKS):
-                for t in range(NEIGHBOURS):
-                    piece = offsets[:, t * PIECE_COLUMNS : (t + 1) * PIECE_COLUMNS]
-                    nc.tensor.matmul(
-                        banks[mb][:],
-                        w_blocks[kb][:, mb * P : (mb + 1) * P],
-                        table_blocks[kb][:].indirect(piece),
-                        start=(kb == 0 and t == 0),
-                        stop=(kb == K_BLOCKS - 1 and t == NEIGHBOURS - 1),
-                    )
+            nc.gpsimd.dma_start(gain[:], s.rearrange("(a p) o -> p (a o)", p=P))
+            nc.gpsimd.dma_start(shift[:], b.rearrange("(a p) o -> p (a o)", p=P))
 
         store_queues = [nc.sync, nc.scalar]
         for mb in range(M_BLOCKS):
+            bank = psum.tile([P, LIST], F32, name=f"bank{mb}")
+            for kb in range(K_BLOCKS):
+                nc.tensor.matmul(
+                    bank[:],
+                    w_blocks[kb][:, mb * P : (mb + 1) * P],
+                    table_blocks[kb][:].indirect(offsets[:]),
+                    start=(kb == 0),
+                    stop=(kb == K_BLOCKS - 1),
+                )
+            summed = held.tile([P, NODES], F32, name=f"summed{mb}")
+            nc.vector.tensor_reduce(
+                summed[:], bank[:].rearrange("p (t v) -> p v t", t=NEIGHBOURS), X, ADD
+            )
             result = held.tile([P, NODES], F32, name=f"result{mb}")
             nc.vector.tensor_scalar(
-                result[:], banks[mb][:], gain[:, mb : mb + 1], shift[:, mb : mb + 1], MULT, ADD
+                result[:], summed[:], gain[:, mb : mb + 1], shift[:, mb : mb + 1], MULT, ADD
             )
             store_queues[mb].dma_start(out[mb * P : (mb + 1) * P, :], result[:])

@@ -40,7 +40,7 @@ def tile_gather_matmul_kernel(tc, table, w, s, b, offs, out):
         shift = held.tile([P, M_BLOCKS], F32, name="shift")
         with nc.allow_non_contiguous_dma(reason="one float32 to a partition"):
             nc.gpsimd.dma_start(gain[:], s.rearrange("(a p) o -> p (a o)", p=P))
-            nc.gpsimd.dma_start(shift[:], b.rearrange("(a p) o -> p (a o)", p=P))
+            nc.scalar.dma_start(shift[:], b.rearrange("(a p) o -> p (a o)", p=P))
 
         store_queues = [nc.sync, nc.scalar]
         for mb in range(M_BLOCKS):

@@ -18,6 +18,7 @@ U16 = mybir.dt.uint16
 MULT = mybir.AluOpType.mult
 ADD = mybir.AluOpType.add
 X = mybir.AxisListType.X
+IDENTITY = mybir.ActivationFunctionType.Identity
 
 
 def tile_gather_matmul_kernel(tc, table, w, s, b, offs, out):
@@ -42,7 +43,11 @@ def tile_gather_matmul_kernel(tc, table, w, s, b, offs, out):
             nc.gpsimd.dma_start(gain[:], s.rearrange("(a p) o -> p (a o)", p=P))
             nc.scalar.dma_start(shift[:], b.rearrange("(a p) o -> p (a o)", p=P))
 
-        store_queues = [nc.sync, nc.scalar]
+        dummy_in = held.tile([P, 1], F32, name="dummy_in")
+        dummy_out = held.tile([P, 1], F32, name="dummy_out")
+        nc.vector.memset(dummy_in[:], 0.0)
+        nc.scalar.activation(dummy_out[:], dummy_in[:], IDENTITY)
+
         for mb in range(M_BLOCKS):
             bank = psum.tile([P, LIST], F32, name=f"bank{mb}")
             for kb in range(K_BLOCKS):
@@ -58,7 +63,14 @@ def tile_gather_matmul_kernel(tc, table, w, s, b, offs, out):
                 summed[:], bank[:].rearrange("p (t v) -> p v t", t=NEIGHBOURS), X, ADD
             )
             result = held.tile([P, NODES], F32, name=f"result{mb}")
-            nc.vector.tensor_scalar(
-                result[:], summed[:], gain[:, mb : mb + 1], shift[:, mb : mb + 1], MULT, ADD
-            )
-            store_queues[mb].dma_start(out[mb * P : (mb + 1) * P, :], result[:])
+            rows = out[mb * P : (mb + 1) * P, :]
+            if mb == 0:
+                nc.scalar.activation(
+                    result[:], summed[:], IDENTITY, bias=shift[:, 0:1], scale=gain[:, 0:1]
+                )
+                nc.scalar.dma_start(rows, result[:])
+            else:
+                nc.vector.tensor_scalar(
+                    result[:], summed[:], gain[:, mb : mb + 1], shift[:, mb : mb + 1], MULT, ADD
+                )
+                nc.sync.dma_start(rows, result[:])

@@ -34,8 +34,8 @@ def tile_gather_matmul_kernel(tc, table, w, s, b, offs, out):
         w_blocks = [held.tile([P, M], BF16, name=f"w{kb}") for kb in range(K_BLOCKS)]
         for kb in range(K_BLOCKS):
             rows = slice(kb * P, (kb + 1) * P)
-            nc.sync.dma_start(table_blocks[kb][:], table[rows, :])
-            nc.scalar.dma_start(w_blocks[kb][:], w[rows, :])
+            nc.scalar.dma_start(table_blocks[kb][:], table[rows, :])
+            nc.sync.dma_start(w_blocks[kb][:], w[rows, :])
 
         gain = held.tile([P, M_BLOCKS], F32, name="gain")
         shift = held.tile([P, M_BLOCKS], F32, name="shift")

@@ -41,7 +41,7 @@ def tile_gather_matmul_kernel(tc, table, w, s, b, offs, out):
         shift = held.tile([P, M_BLOCKS], F32, name="shift")
         with nc.allow_non_contiguous_dma(reason="one float32 to a partition"):
             nc.gpsimd.dma_start(gain[:], s.rearrange("(a p) o -> p (a o)", p=P))
-            nc.scalar.dma_start(shift[:], b.rearrange("(a p) o -> p (a o)", p=P))
+            nc.sync.dma_start(shift[:], b.rearrange("(a p) o -> p (a o)", p=P))
 
         dummy_in = held.tile([P, 1], F32, name="dummy_in")
         dummy_out = held.tile([P, 1], F32, name="dummy_out")

@@ -73,4 +73,4 @@ def tile_gather_matmul_kernel(tc, table, w, s, b, offs, out):
                 nc.vector.tensor_scalar(
                     result[:], summed[:], gain[:, mb : mb + 1], shift[:, mb : mb + 1], MULT, ADD
                 )
-                nc.sync.dma_start(rows, result[:])
+                nc.scalar.dma_start(rows, result[:])

import concourse.mybir as mybir

P = 128
S = 512
K = 256
M = 256
NEIGHBOURS = 4
NODES = 64
LIST = NEIGHBOURS * NODES
K_BLOCKS = K // P
M_BLOCKS = M // P

FLOPS = 2 * K * M * NODES + (NEIGHBOURS - 1) * K * NODES + 2 * M * NODES

BF16 = mybir.dt.bfloat16
F32 = mybir.dt.float32
U16 = mybir.dt.uint16
MULT = mybir.AluOpType.mult
ADD = mybir.AluOpType.add
X = mybir.AxisListType.X
IDENTITY = mybir.ActivationFunctionType.Identity


def tile_gather_matmul_kernel(tc, table, w, s, b, offs, out):
    nc = tc.nc
    with (
        tc.tile_pool(name="held", bufs=1) as held,
        tc.psum_pool(name="psum", bufs=1) as psum,
    ):
        offsets = held.tile([P, LIST // 16], U16, name="offsets")
        nc.sync.dma_start(offsets[:], offs)

        table_blocks = [held.tile([P, S], BF16, name=f"table{kb}") for kb in range(K_BLOCKS)]
        w_blocks = [held.tile([P, M], BF16, name=f"w{kb}") for kb in range(K_BLOCKS)]
        for kb in range(K_BLOCKS):
            rows = slice(kb * P, (kb + 1) * P)
            nc.scalar.dma_start(table_blocks[kb][:], table[rows, :])
            nc.sync.dma_start(w_blocks[kb][:], w[rows, :])

        gain = held.tile([P, M_BLOCKS], F32, name="gain")
        shift = held.tile([P, M_BLOCKS], F32, name="shift")
        with nc.allow_non_contiguous_dma(reason="one float32 to a partition"):
            nc.gpsimd.dma_start(gain[:], s.rearrange("(a p) o -> p (a o)", p=P))
            nc.sync.dma_start(shift[:], b.rearrange("(a p) o -> p (a o)", p=P))

        dummy_in = held.tile([P, 1], F32, name="dummy_in")
        dummy_out = held.tile([P, 1], F32, name="dummy_out")
        nc.vector.memset(dummy_in[:], 0.0)
        nc.scalar.activation(dummy_out[:], dummy_in[:], IDENTITY)

        for mb in range(M_BLOCKS):
            bank = psum.tile([P, LIST], F32, name=f"bank{mb}")
            for kb in range(K_BLOCKS):
                nc.tensor.matmul(
                    bank[:],
                    w_blocks[kb][:, mb * P : (mb + 1) * P],
                    table_blocks[kb][:].indirect(offsets[:]),
                    start=(kb == 0),
                    stop=(kb == K_BLOCKS - 1),
                )
            summed = held.tile([P, NODES], F32, name=f"summed{mb}")
            nc.vector.tensor_reduce(
                summed[:], bank[:].rearrange("p (t v) -> p v t", t=NEIGHBOURS), X, ADD
            )
            result = held.tile([P, NODES], F32, name=f"result{mb}")
            rows = out[mb * P : (mb + 1) * P, :]
            if mb == 0:
                nc.scalar.activation(
                    result[:], summed[:], IDENTITY, bias=shift[:, 0:1], scale=gain[:, 0:1]
                )
                nc.scalar.dma_start(rows, result[:])
            else:
                nc.vector.tensor_scalar(
                    result[:], summed[:], gain[:, mb : mb + 1], shift[:, mb : mb + 1], MULT, ADD
                )
                nc.scalar.dma_start(rows, result[:])
